import numpy as np
import ml_dtypes


def mxq(x, axis, fmt="e4m3"):
    dtype, down = {"e4m3": (ml_dtypes.float8_e4m3fn, 7), "e5m2": (ml_dtypes.float8_e5m2, 14)}[fmt]
    v = np.moveaxis(np.asarray(x, np.float32).astype(ml_dtypes.bfloat16).astype(np.float64), axis, -1)
    blocks = v.reshape(v.shape[:-1] + (-1, 32))
    amax = np.abs(blocks).max(-1, keepdims=True)
    byte = np.maximum(np.where(amax > 0, np.frexp(amax)[1] - 1 + 127, 0) - down, 1)
    scale = np.exp2(byte - 127.0)
    codes = (blocks / scale).astype(np.float32).astype(dtype).astype(np.float64)
    return np.moveaxis((codes * scale).reshape(v.shape), -1, axis)


WIDE = False


def mx_kscale(k):
    if not WIDE:
        return np.ones(k)
    levels = np.array([30, -30])
    if k % 512:
        return np.exp2(np.random.permutation(np.resize(levels, k // 32))).repeat(32)
    a = np.empty((k // 512, 16))
    for p in range(k // 512):
        a[p, :8] = np.random.permutation(np.resize(levels, 8))
        for g in range(8):
            far = levels[np.abs(levels - a[p, g]) >= 10]
            a[p, g + 8] = far[np.random.randint(len(far))]
    return np.exp2(a.ravel()).repeat(32)


def f64(x):
    return np.asarray(x).astype(np.float64)


def striped(idx):
    return np.tile(np.asarray(idx).reshape(-1, 16).T, (8, 1)).astype(np.uint16)


def unstriped(offs):
    return offs[:16].T.reshape(-1).astype(np.int64)


E2M1 = np.array([0.0, 0.5, 1.0, 1.5, 2.0, 3.0, 4.0, 6.0, -0.0, -0.5, -1.0, -1.5, -2.0, -3.0, -4.0, -6.0])


def pack_weight(w, fmt):
    k, n = w.shape
    w = f64(np.asarray(w, np.float32).astype(ml_dtypes.bfloat16)).reshape(k // 32, 32, n)
    amax = np.abs(w).max(1)
    if fmt in ("e4m3", "e5m2"):
        byte = np.frexp(amax)[1] - 1 + 127 - (7 if fmt == "e4m3" else 14)
    else:
        mant, ex = np.frexp(amax / 6.0)
        byte = np.where(mant > 0.5, ex, ex - 1) + 127
    byte = np.clip(np.where(amax > 0, byte, 1), 1, 254)
    scaled = (w * np.exp2(127.0 - byte)[:, None, :]).reshape(k, n).astype(np.float32)
    by_word = np.ascontiguousarray(scaled.reshape(k // 512, 128, 4, n).transpose(0, 1, 3, 2))
    if fmt in ("e4m3", "e5m2"):
        words = by_word.astype(ml_dtypes.float8_e4m3fn if fmt == "e4m3" else ml_dtypes.float8_e5m2).view(np.uint8)
    else:
        c = by_word.astype(ml_dtypes.float4_e2m1fn).view(np.uint8) & 0xF
        words = (c[..., 0::2] | (c[..., 1::2] << 4)).reshape(k // 512, 128, 2 * n)
    return np.ascontiguousarray(words), np.ascontiguousarray(byte.astype(np.uint8).reshape(k // 512, 16, n))


def unpack_weight(words, scales, fmt):
    g, _, n = scales.shape
    words = np.ascontiguousarray(words).reshape(g, 128, n, -1)
    if fmt in ("e4m3", "e5m2"):
        vals = words.view(ml_dtypes.float8_e4m3fn if fmt == "e4m3" else ml_dtypes.float8_e5m2).astype(np.float64)
    else:
        nib = np.empty((g, 128, n, 4), np.uint8)
        nib[..., 0::2] = words & 0xF
        nib[..., 1::2] = words >> 4
        vals = E2M1[nib]
    vals = vals * np.repeat(np.exp2(scales.astype(np.float64) - 127.0), 8, axis=1)[..., None]
    return vals.transpose(0, 1, 3, 2).reshape(g * 512, n)


def e4m3fn_bytes(y):
    return np.clip(np.asarray(y, np.float64), -448.0, 448.0).astype(np.float32).astype(ml_dtypes.float8_e4m3fn).view(np.uint8)


def e4m3fn_values(b):
    return np.asarray(b, np.uint8).view(ml_dtypes.float8_e4m3fn).astype(np.float64)


K, T, J, R, F, Z, N, V, O = 512, 1024, 256, 512, 512, 1024, 256, 1024, 128


def setup_inputs():
    n = np.random.standard_normal
    idx = np.random.permutation(T)[:J]
    idx2 = np.random.permutation(Z)[:J]
    idx3 = np.random.permutation(V)[:N]
    idx4 = np.random.permutation(J)[:O]
    fk = mx_kscale(K)
    ff = mx_kscale(F)
    fr = mx_kscale(R)
    xtp = pack_weight(n((K, T)) / fk[:, None], "e4m3")
    xop = pack_weight(n((F, Z)) / ff[:, None], "e2m1")
    wp = pack_weight(n((K, R)) * 1 / np.sqrt(K) * fk[:, None], "e2m1")
    w0p = pack_weight(n((F, R)) * 1 / np.sqrt(F) * ff[:, None], "e5m2")
    return {
        "xt_words": xtp[0],
        "xt_scales": xtp[1],
        "xo_words": xop[0],
        "xo_scales": xop[1],
        "w_words": wp[0],
        "w_scales": wp[1],
        "w0_words": w0p[0],
        "w0_scales": w0p[1],
        "ca": e4m3fn_bytes(60.0 * n((R, V))),
        "sw": (np.random.uniform(0.0004, 0.0012, (R, 1)) / fr[:, None]).astype(np.float32),
        "sa": (np.random.uniform(0.5, 1.6, (R, 1)) * fr[:, None]).astype(np.float32),
        "offs": striped(idx),
        "offs2": striped(idx2),
        "offs3": striped(idx3),
        "offs4": striped(idx4),
    }


def reference(xt_words, xt_scales, xo_words, xo_scales, w_words, w_scales, w0_words, w0_scales, ca, sw, sa, offs, offs2, offs3, offs4):
    idx = unstriped(offs)
    idx2 = unstriped(offs2)
    idx3 = unstriped(offs3)
    idx4 = unstriped(offs4)
    xtu = unpack_weight(xt_words, xt_scales, "e4m3")
    xou = unpack_weight(xo_words, xo_scales, "e2m1")
    wu = unpack_weight(w_words, w_scales, "e2m1")
    w0u = unpack_weight(w0_words, w0_scales, "e5m2")
    xtidxg = xtu[:, idx]
    xoidx2g = xou[:, idx2]
    a = wu.T @ xtidxg + w0u.T @ xoidx2g
    wq = e4m3fn_values(ca)[:, idx3] * f64(sw)
    g1 = np.maximum(a, 0.0)
    hid = g1[:, idx4] * f64(sa)
    wqq = mxq(wq, 0, "e4m3")
    hidq = mxq(hid, 0, "e4m3")
    p = wqq.T @ hidq
    return p

@@ -1,0 +1,139 @@
+from contextlib import ExitStack
+
+import concourse.mybir as mybir
+
+F32 = mybir.dt.float32
+BF16 = mybir.dt.bfloat16
+I32 = mybir.dt.int32
+U32 = mybir.dt.uint32
+U16 = mybir.dt.uint16
+U8 = mybir.dt.uint8
+FP8 = mybir.dt.float8_e4m3fn
+E4M3X4 = mybir.dt.float8_e4m3fn_x4
+E5M2X4 = mybir.dt.float8_e5m2_x4
+E2M1X4 = mybir.dt.float4_e2m1fn_x4
+ACT = mybir.ActivationFunctionType
+
+P = 128
+PACK = 4
+T, J, R, Z, N, V, O = 1024, 256, 512, 1024, 256, 1024, 128
+FLOPS = 2 * (512 * R * J + 512 * R * J + R * N * O)
+
+
+def tile_list_codedcolumns_kernel(
+    tc, xt_words, xt_scales, xo_words, xo_scales, w_words, w_scales, w0_words, w0_scales,
+    ca, sw, sa, offs, offs2, offs3, offs4, out,
+):
+    nc = tc.nc
+    with ExitStack() as ctx:
+        sb = ctx.enter_context(tc.tile_pool(name="sb", bufs=1))
+        ps = ctx.enter_context(tc.psum_pool(name="ps", bufs=1))
+
+        def tile(name, shape, dtype, tag=None):
+            return sb.tile(shape, dtype, name=name, tag=tag or name, align_bytes=64)
+
+        def load_list(name, src, queue_cols):
+            t = tile(name, [P, queue_cols], U16)
+            nc.sync.dma_start(t[:], src)
+            return t
+
+        def plane(name, width, engine):
+            t = tile(name, [P, width], U8)
+            engine.memset(t[:].bitcast(I32), 0)
+            return t
+
+        def load_plane(queue, t, src):
+            for q in range(4):
+                queue.dma_start(t[32 * q : 32 * q + 4, :].bitcast(I32), src[0, 4 * q : 4 * q + 4, :].bitcast(I32))
+
+        ws_raw = plane("ws_raw", R, nc.gpsimd)
+        xts_win = plane("xts_win", T, nc.vector)
+        xos_win = plane("xos_win", Z, nc.vector)
+        w0s_raw = plane("w0s_raw", R, nc.vector)
+
+        load_plane(nc.gpsimd, ws_raw, w_scales)
+
+        ca_rows = ca.rearrange("(p t) v -> t p v", t=PACK)
+        ca_win = [tile("ca_win%d" % t, [P, V], U8) for t in range(PACK)]
+        l3 = load_list("l3", offs3, N // 16)
+        nc.sync.dma_start(ca_win[0][:], ca_rows[0])
+        nc.sync.dma_start(ca_win[1][:], ca_rows[1])
+        sw_sb = tile("sw_sb", [P, PACK], F32)
+        nc.sync.dma_start(sw_sb[:], sw.rearrange("(p t) o -> p (t o)", t=PACK))
+        nc.sync.dma_start(ca_win[2][:], ca_rows[2])
+        nc.sync.dma_start(ca_win[3][:], ca_rows[3])
+        l1 = load_list("l1", offs, J // 16)
+        xt_win = tile("xt_win", [P, T], U32)
+        nc.sync.dma_start(xt_win[:].bitcast(I32), xt_words[0].rearrange("p c r -> p (c r)").bitcast(I32))
+        load_plane(nc.sync, xts_win, xt_scales)
+        l2 = load_list("l2", offs2, J // 16)
+        xo_win = tile("xo_win", [P, Z], U16)
+        nc.sync.dma_start(xo_win[:].bitcast(I32), xo_words[0].bitcast(I32))
+        w_raw = tile("w_raw", [P, R], U16)
+        nc.sync.dma_start(w_raw[:].bitcast(I32), w_words[0].bitcast(I32))
+        w0_raw = tile("w0_raw", [P, R], U32)
+        nc.sync.dma_start(w0_raw[:].bitcast(I32), w0_words[0].rearrange("p c r -> p (c r)").bitcast(I32))
+        load_plane(nc.sync, xos_win, xo_scales)
+        load_plane(nc.sync, w0s_raw, w0_scales)
+        l4 = load_list("l4", offs4, O // 16)
+        sa_sb = tile("sa_sb", [P, PACK], F32)
+        nc.sync.dma_start(sa_sb[:], sa.rearrange("(p t) o -> p (t o)", t=PACK))
+
+        ca_got = tile("ca_got", [P, PACK, N], U8)
+        wq4 = tile("wq4", [P, PACK, N], BF16)
+        for t in range(PACK):
+            nc.vector.tensor_copy(ca_got[:, t, :], ca_win[t][:].indirect(l3[:]))
+            nc.scalar.activation(wq4[:, t, :], ca_got[:, t, :].bitcast(FP8), ACT.Copy, scale=sw_sb[:, t : t + 1])
+        wq_il = tile("wq_il", [P, N, PACK], BF16)
+        nc.scalar.copy(wq_il[:], wq4[:].rearrange("p t n -> p n t"))
+
+        xts_got = tile("xts_got", [P, J], U8)
+        xt_got = tile("xt_got", [P, J], U32)
+        xo_got = tile("xo_got", [P, J], U16)
+        xos_got = tile("xos_got", [P, J], U8)
+        nc.vector.tensor_copy(xts_got[:], xts_win[:].indirect(l1[:]))
+        nc.vector.tensor_copy(xt_got[:], xt_win[:].indirect(l1[:]))
+        nc.vector.tensor_copy(xo_got[:], xo_win[:].indirect(l2[:]))
+        nc.vector.tensor_copy(xos_got[:], xos_win[:].indirect(l2[:]))
+
+        def deal(copy, name, raw, dtype, tag=None):
+            t = tile(name, [P, PACK, P], dtype, tag)
+            copy(t[:], raw[:].rearrange("p (q t) -> p t q", t=PACK))
+            return t
+
+        w_d = deal(nc.scalar.copy, "w_d", w_raw, U16)
+        w0_d = deal(nc.scalar.copy, "w0_d", w0_raw, U32)
+        ws_d = deal(nc.vector.tensor_copy, "ws_d", ws_raw, U8, "xt_win")
+        w0s_d = deal(nc.vector.tensor_copy, "w0s_d", w0s_raw, U8)
+
+        acc = [ps.tile([P, J], F32, name="acc%d" % t) for t in range(PACK)]
+        for t in range(PACK):
+            nc.tensor.matmul_mx(acc[t][:], lhsT=w_d[:, t, :].bitcast(E2M1X4), lhsT_scale=ws_d[:, t, :],
+                                rhs=xt_got[:].bitcast(E4M3X4), rhs_scale=xts_got[:], start=True, stop=False)
+        for t in range(PACK):
+            nc.tensor.matmul_mx(acc[t][:], lhsT=w0_d[:, t, :].bitcast(E5M2X4), lhsT_scale=w0s_d[:, t, :],
+                                rhs=xo_got[:].bitcast(E2M1X4), rhs_scale=xos_got[:], start=False, stop=True)
+
+        wq_codes = tile("wq_codes", [P, N], U32)
+        wq_scales = tile("wq_scales", [P, N], U8)
+        nc.vector.quantize_mx(wq_codes[:].bitcast(E4M3X4), wq_scales[:], wq_il[:].rearrange("p n t -> p (n t)"))
+
+        hid4 = tile("hid4", [P, PACK, O], BF16)
+        for t in range(PACK):
+            g1 = tile("g1_%d" % t, [P, J], F32)
+            nc.vector.tensor_scalar_max(g1[:], acc[t][:], 0.0)
+            nc.scalar.activation(hid4[:, t, :], g1[:].indirect(l4[:]), ACT.Copy, scale=sa_sb[:, t : t + 1])
+        hid_il = tile("hid_il", [P, O, PACK], BF16)
+        nc.vector.tensor_copy(hid_il[:], hid4[:].rearrange("p t o -> p o t"))
+        hid_codes = tile("hid_codes", [P, O], U32)
+        hid_scales = tile("hid_scales", [P, O], U8)
+        nc.vector.quantize_mx(hid_codes[:].bitcast(E4M3X4), hid_scales[:], hid_il[:].rearrange("p o t -> p (o t)"))
+
+        for h, (copy, queue) in enumerate(((nc.vector.tensor_copy, nc.sync), (nc.scalar.copy, nc.scalar))):
+            cols = slice(h * P, (h + 1) * P)
+            res = ps.tile([P, O], F32, name="res%d" % h)
+            nc.tensor.matmul_mx(res[:], lhsT=wq_codes[:, cols].bitcast(E4M3X4), lhsT_scale=wq_scales[:, cols],
+                                rhs=hid_codes[:].bitcast(E4M3X4), rhs_scale=hid_scales[:], start=True, stop=True)
+            res_sb = tile("res_sb%d" % h, [P, O], F32)
+            copy(res_sb[:], res[:])
+            queue.dma_start(out[cols, :], res_sb[:])

@@ -37,84 +37,96 @@ def tile_list_codedcolumns_kernel(
             nc.sync.dma_start(t[:], src)
             return t
 
-        def plane(name, width, engine):
-            t = tile(name, [P, width], U8)
-            engine.memset(t[:].bitcast(I32), 0)
+        def stage(name, width, engine):
+            t = tile(name, [P, 2, width], U8)
+            engine.memset(t[:].rearrange("p a c -> p (a c)").bitcast(I32), 0)
             return t
 
-        def load_plane(queue, t, src):
-            for q in range(4):
-                queue.dma_start(t[32 * q : 32 * q + 4, :].bitcast(I32), src[0, 4 * q : 4 * q + 4, :].bitcast(I32))
+        def load_stage(queue, t, src):
+            rows = src[0].rearrange("(a b r) c -> b r a c", a=2, b=2)
+            for b in range(2):
+                queue.dma_start(t[32 * b : 32 * b + 4, :, :].bitcast(I32), rows[b].bitcast(I32))
 
-        ws_raw = plane("ws_raw", R, nc.gpsimd)
-        xts_win = plane("xts_win", T, nc.vector)
-        xos_win = plane("xos_win", Z, nc.vector)
-        w0s_raw = plane("w0s_raw", R, nc.vector)
-
-        load_plane(nc.gpsimd, ws_raw, w_scales)
+        w0s_raw = stage("w0s_raw", R, nc.vector)
+        xos_raw = stage("xos_raw", Z, nc.vector)
+        ws_raw = stage("ws_raw", R, nc.gpsimd)
+        xts_raw = stage("xts_raw", T, nc.gpsimd)
 
         ca_rows = ca.rearrange("(p t) v -> t p v", t=PACK)
         ca_win = [tile("ca_win%d" % t, [P, V], U8) for t in range(PACK)]
-        l3 = load_list("l3", offs3, N // 16)
         nc.sync.dma_start(ca_win[0][:], ca_rows[0])
-        nc.sync.dma_start(ca_win[1][:], ca_rows[1])
         sw_sb = tile("sw_sb", [P, PACK], F32)
-        nc.sync.dma_start(sw_sb[:], sw.rearrange("(p t) o -> p (t o)", t=PACK))
-        nc.sync.dma_start(ca_win[2][:], ca_rows[2])
-        nc.sync.dma_start(ca_win[3][:], ca_rows[3])
-        l1 = load_list("l1", offs, J // 16)
-        xt_win = tile("xt_win", [P, T], U32)
-        nc.sync.dma_start(xt_win[:].bitcast(I32), xt_words[0].rearrange("p c r -> p (c r)").bitcast(I32))
-        load_plane(nc.sync, xts_win, xt_scales)
+        nc.scalar.dma_start(sw_sb[:], sw.rearrange("(p t) o -> p (t o)", t=PACK))
+        l3 = load_list("l3", offs3, N // 16)
+        load_stage(nc.scalar, w0s_raw, w0_scales)
+        for t in range(1, PACK):
+            nc.sync.dma_start(ca_win[t][:], ca_rows[t])
+        load_stage(nc.sync, xos_raw, xo_scales)
+        load_stage(nc.sync, ws_raw, w_scales)
         l2 = load_list("l2", offs2, J // 16)
         xo_win = tile("xo_win", [P, Z], U16)
         nc.sync.dma_start(xo_win[:].bitcast(I32), xo_words[0].bitcast(I32))
-        w_raw = tile("w_raw", [P, R], U16)
-        nc.sync.dma_start(w_raw[:].bitcast(I32), w_words[0].bitcast(I32))
         w0_raw = tile("w0_raw", [P, R], U32)
         nc.sync.dma_start(w0_raw[:].bitcast(I32), w0_words[0].rearrange("p c r -> p (c r)").bitcast(I32))
-        load_plane(nc.sync, xos_win, xo_scales)
-        load_plane(nc.sync, w0s_raw, w0_scales)
+        w_raw = tile("w_raw", [P, R], U16)
+        nc.sync.dma_start(w_raw[:].bitcast(I32), w_words[0].bitcast(I32))
+        load_stage(nc.sync, xts_raw, xt_scales)
+        l1 = load_list("l1", offs, J // 16)
+        xt_win = tile("xt_win", [P, T], U32)
+        nc.sync.dma_start(xt_win[:].bitcast(I32), xt_words[0].rearrange("p c r -> p (c r)").bitcast(I32))
         l4 = load_list("l4", offs4, O // 16)
         sa_sb = tile("sa_sb", [P, PACK], F32)
         nc.sync.dma_start(sa_sb[:], sa.rearrange("(p t) o -> p (t o)", t=PACK))
+
+        def lift(raw):
+            nc.vector.tensor_copy(raw[64:128, 0, :].bitcast(I32), raw[0:64, 1, :].bitcast(I32))
+
+        def spread(name, raw, width):
+            t = tile(name, [P, width], U8)
+            for a in range(2):
+                nc.vector.tensor_copy(t[64 * a : 64 * a + 64, :].bitcast(I32), raw[0:64, a, :].bitcast(I32))
+            return t
 
         ca_got = tile("ca_got", [P, PACK, N], U8)
         wq4 = tile("wq4", [P, PACK, N], BF16)
         for t in range(PACK):
             nc.vector.tensor_copy(ca_got[:, t, :], ca_win[t][:].indirect(l3[:]))
             nc.scalar.activation(wq4[:, t, :], ca_got[:, t, :].bitcast(FP8), ACT.Copy, scale=sw_sb[:, t : t + 1])
-        wq_il = tile("wq_il", [P, N, PACK], BF16)
-        nc.scalar.copy(wq_il[:], wq4[:].rearrange("p t n -> p n t"))
 
         xts_got = tile("xts_got", [P, J], U8)
         xt_got = tile("xt_got", [P, J], U32)
         xo_got = tile("xo_got", [P, J], U16)
         xos_got = tile("xos_got", [P, J], U8)
+        lift(w0s_raw)
+        xos_win = spread("xos_win", xos_raw, Z)
+        lift(ws_raw)
+        nc.vector.tensor_copy(xos_got[:], xos_win[:].indirect(l2[:]))
+        nc.vector.tensor_copy(xo_got[:], xo_win[:].indirect(l2[:]))
+        xts_win = spread("xts_win", xts_raw, T)
         nc.vector.tensor_copy(xts_got[:], xts_win[:].indirect(l1[:]))
         nc.vector.tensor_copy(xt_got[:], xt_win[:].indirect(l1[:]))
-        nc.vector.tensor_copy(xo_got[:], xo_win[:].indirect(l2[:]))
-        nc.vector.tensor_copy(xos_got[:], xos_win[:].indirect(l2[:]))
 
-        def deal(copy, name, raw, dtype, tag=None):
-            t = tile(name, [P, PACK, P], dtype, tag)
-            copy(t[:], raw[:].rearrange("p (q t) -> p t q", t=PACK))
+        def deal(copy, name, raw, dtype, run):
+            t = tile(name, [P, PACK, P], dtype)
+            copy(t[:].rearrange("p t (c i) -> p c t i", i=run), raw.rearrange("p (c i t) -> p c t i", t=PACK, i=run))
             return t
 
-        w_d = deal(nc.scalar.copy, "w_d", w_raw, U16)
-        w0_d = deal(nc.scalar.copy, "w0_d", w0_raw, U32)
-        ws_d = deal(nc.vector.tensor_copy, "ws_d", ws_raw, U8, "xt_win")
-        w0s_d = deal(nc.vector.tensor_copy, "w0s_d", w0s_raw, U8)
+        w0_d = deal(nc.scalar.copy, "w0_d", w0_raw[:], U32, 4)
+        wq_il = tile("wq_il", [P, N, PACK], BF16, "w0_raw")
+        nc.scalar.copy(wq_il[:], wq4[:].rearrange("p t n -> p n t"))
+        w_d = deal(nc.scalar.copy, "w_d", w_raw[:], U16, 8)
+        w0s_d = deal(nc.gpsimd.tensor_copy, "w0s_d", w0s_raw[:, 0, :], U8, P)
+        ws_d = deal(nc.gpsimd.tensor_copy, "ws_d", ws_raw[:, 0, :], U8, P)
 
         acc = [ps.tile([P, J], F32, name="acc%d" % t) for t in range(PACK)]
         for t in range(PACK):
-            nc.tensor.matmul_mx(acc[t][:], lhsT=w_d[:, t, :].bitcast(E2M1X4), lhsT_scale=ws_d[:, t, :],
-                                rhs=xt_got[:].bitcast(E4M3X4), rhs_scale=xts_got[:], start=True, stop=False)
-        for t in range(PACK):
             nc.tensor.matmul_mx(acc[t][:], lhsT=w0_d[:, t, :].bitcast(E5M2X4), lhsT_scale=w0s_d[:, t, :],
-                                rhs=xo_got[:].bitcast(E2M1X4), rhs_scale=xos_got[:], start=False, stop=True)
+                                rhs=xo_got[:].bitcast(E2M1X4), rhs_scale=xos_got[:], start=True, stop=False)
+        for t in range(PACK):
+            nc.tensor.matmul_mx(acc[t][:], lhsT=w_d[:, t, :].bitcast(E2M1X4), lhsT_scale=ws_d[:, t, :],
+                                rhs=xt_got[:].bitcast(E4M3X4), rhs_scale=xts_got[:], start=False, stop=True)
 
-        wq_codes = tile("wq_codes", [P, N], U32)
+        wq_codes = tile("wq_codes", [P, N], U32, "xt_win")
         wq_scales = tile("wq_scales", [P, N], U8)
         nc.vector.quantize_mx(wq_codes[:].bitcast(E4M3X4), wq_scales[:], wq_il[:].rearrange("p n t -> p (n t)"))
 

@@ -47,10 +47,21 @@ def tile_list_codedcolumns_kernel(
             for b in range(2):
                 queue.dma_start(t[32 * b : 32 * b + 4, :, :].bitcast(I32), rows[b].bitcast(I32))
 
-        w0s_raw = stage("w0s_raw", R, nc.vector)
-        xos_raw = stage("xos_raw", Z, nc.vector)
-        ws_raw = stage("ws_raw", R, nc.gpsimd)
-        xts_raw = stage("xts_raw", T, nc.gpsimd)
+        def plane(name, width):
+            t = tile(name, [P, width], U8)
+            nc.vector.memset(t[:].bitcast(I32), 0)
+            return t
+
+        def load_plane(t, src):
+            for q in range(4):
+                nc.sync.dma_start(t[32 * q : 32 * q + 4, :].bitcast(I32), src[0, 4 * q : 4 * q + 4, :].bitcast(I32))
+
+        w0s_raw = stage("w0s_raw", R, nc.gpsimd)
+        ws_raw = stage("ws_raw", R, nc.vector)
+        xos_win = plane("xos_win", Z)
+        xts_win = plane("xts_win", T)
+        load_stage(nc.gpsimd, w0s_raw, w0_scales)
+        load_stage(nc.gpsimd, ws_raw, w_scales)
 
         ca_rows = ca.rearrange("(p t) v -> t p v", t=PACK)
         ca_win = [tile("ca_win%d" % t, [P, V], U8) for t in range(PACK)]
@@ -58,31 +69,26 @@ def tile_list_codedcolumns_kernel(
         sw_sb = tile("sw_sb", [P, PACK], F32)
         nc.scalar.dma_start(sw_sb[:], sw.rearrange("(p t) o -> p (t o)", t=PACK))
         l3 = load_list("l3", offs3, N // 16)
-        load_stage(nc.scalar, w0s_raw, w0_scales)
         for t in range(1, PACK):
             nc.sync.dma_start(ca_win[t][:], ca_rows[t])
-        load_stage(nc.sync, xos_raw, xo_scales)
-        load_stage(nc.sync, ws_raw, w_scales)
-        l2 = load_list("l2", offs2, J // 16)
         xo_win = tile("xo_win", [P, Z], U16)
         nc.sync.dma_start(xo_win[:].bitcast(I32), xo_words[0].bitcast(I32))
         w0_raw = tile("w0_raw", [P, R], U32)
         nc.sync.dma_start(w0_raw[:].bitcast(I32), w0_words[0].rearrange("p c r -> p (c r)").bitcast(I32))
-        w_raw = tile("w_raw", [P, R], U16)
-        nc.sync.dma_start(w_raw[:].bitcast(I32), w_words[0].bitcast(I32))
-        load_stage(nc.sync, xts_raw, xt_scales)
-        l1 = load_list("l1", offs, J // 16)
+        l2 = load_list("l2", offs2, J // 16)
+        load_plane(xos_win, xo_scales)
         xt_win = tile("xt_win", [P, T], U32)
         nc.sync.dma_start(xt_win[:].bitcast(I32), xt_words[0].rearrange("p c r -> p (c r)").bitcast(I32))
+        l1 = load_list("l1", offs, J // 16)
+        w_raw = tile("w_raw", [P, R], U16)
+        nc.sync.dma_start(w_raw[:].bitcast(I32), w_words[0].bitcast(I32))
+        load_plane(xts_win, xt_scales)
         l4 = load_list("l4", offs4, O // 16)
         sa_sb = tile("sa_sb", [P, PACK], F32)
         nc.sync.dma_start(sa_sb[:], sa.rearrange("(p t) o -> p (t o)", t=PACK))
 
-        def lift(raw):
-            nc.vector.tensor_copy(raw[64:128, 0, :].bitcast(I32), raw[0:64, 1, :].bitcast(I32))
-
-        def spread(name, raw, width):
-            t = tile(name, [P, width], U8)
+        def spread(name, raw, width, tag):
+            t = tile(name, [P, width], U8, tag)
             for a in range(2):
                 nc.vector.tensor_copy(t[64 * a : 64 * a + 64, :].bitcast(I32), raw[0:64, a, :].bitcast(I32))
             return t
@@ -97,14 +103,12 @@ def tile_list_codedcolumns_kernel(
         xt_got = tile("xt_got", [P, J], U32)
         xo_got = tile("xo_got", [P, J], U16)
         xos_got = tile("xos_got", [P, J], U8)
-        lift(w0s_raw)
-        xos_win = spread("xos_win", xos_raw, Z)
-        lift(ws_raw)
-        nc.vector.tensor_copy(xos_got[:], xos_win[:].indirect(l2[:]))
+        w0s_plane = spread("w0s_plane", w0s_raw, R, "ca_win3")
         nc.vector.tensor_copy(xo_got[:], xo_win[:].indirect(l2[:]))
-        xts_win = spread("xts_win", xts_raw, T)
-        nc.vector.tensor_copy(xts_got[:], xts_win[:].indirect(l1[:]))
+        nc.vector.tensor_copy(xos_got[:], xos_win[:].indirect(l2[:]))
+        ws_plane = spread("ws_plane", ws_raw, R, "xos_win")
         nc.vector.tensor_copy(xt_got[:], xt_win[:].indirect(l1[:]))
+        nc.vector.tensor_copy(xts_got[:], xts_win[:].indirect(l1[:]))
 
         def deal(copy, name, raw, dtype, run):
             t = tile(name, [P, PACK, P], dtype)
@@ -115,8 +119,8 @@ def tile_list_codedcolumns_kernel(
         wq_il = tile("wq_il", [P, N, PACK], BF16, "w0_raw")
         nc.scalar.copy(wq_il[:], wq4[:].rearrange("p t n -> p n t"))
         w_d = deal(nc.scalar.copy, "w_d", w_raw[:], U16, 8)
-        w0s_d = deal(nc.gpsimd.tensor_copy, "w0s_d", w0s_raw[:, 0, :], U8, P)
-        ws_d = deal(nc.gpsimd.tensor_copy, "ws_d", ws_raw[:, 0, :], U8, P)
+        w0s_d = deal(nc.gpsimd.tensor_copy, "w0s_d", w0s_plane[:], U8, P)
+        ws_d = deal(nc.gpsimd.tensor_copy, "ws_d", ws_plane[:], U8, P)
 
         acc = [ps.tile([P, J], F32, name="acc%d" % t) for t in range(PACK)]
         for t in range(PACK):
@@ -126,7 +130,7 @@ def tile_list_codedcolumns_kernel(
             nc.tensor.matmul_mx(acc[t][:], lhsT=w_d[:, t, :].bitcast(E2M1X4), lhsT_scale=ws_d[:, t, :],
                                 rhs=xt_got[:].bitcast(E4M3X4), rhs_scale=xts_got[:], start=False, stop=True)
 
-        wq_codes = tile("wq_codes", [P, N], U32, "xt_win")
+        wq_codes = tile("wq_codes", [P, N], U32, "xts_win")
         wq_scales = tile("wq_scales", [P, N], U8)
         nc.vector.quantize_mx(wq_codes[:].bitcast(E4M3X4), wq_scales[:], wq_il[:].rearrange("p n t -> p (n t)"))
 

from contextlib import ExitStack

import concourse.mybir as mybir

F32 = mybir.dt.float32
BF16 = mybir.dt.bfloat16
I32 = mybir.dt.int32
U32 = mybir.dt.uint32
U16 = mybir.dt.uint16
U8 = mybir.dt.uint8
FP8 = mybir.dt.float8_e4m3fn
E4M3X4 = mybir.dt.float8_e4m3fn_x4
E5M2X4 = mybir.dt.float8_e5m2_x4
E2M1X4 = mybir.dt.float4_e2m1fn_x4
ACT = mybir.ActivationFunctionType

P = 128
PACK = 4
T, J, R, Z, N, V, O = 1024, 256, 512, 1024, 256, 1024, 128
FLOPS = 2 * (512 * R * J + 512 * R * J + R * N * O)


def tile_list_codedcolumns_kernel(
    tc, xt_words, xt_scales, xo_words, xo_scales, w_words, w_scales, w0_words, w0_scales,
    ca, sw, sa, offs, offs2, offs3, offs4, out,
):
    nc = tc.nc
    with ExitStack() as ctx:
        sb = ctx.enter_context(tc.tile_pool(name="sb", bufs=1))
        ps = ctx.enter_context(tc.psum_pool(name="ps", bufs=1))

        def tile(name, shape, dtype, tag=None):
            return sb.tile(shape, dtype, name=name, tag=tag or name, align_bytes=64)

        def load_list(name, src, queue_cols):
            t = tile(name, [P, queue_cols], U16)
            nc.sync.dma_start(t[:], src)
            return t

        def stage(name, width, engine):
            t = tile(name, [P, 2, width], U8)
            engine.memset(t[:].rearrange("p a c -> p (a c)").bitcast(I32), 0)
            return t

        def load_stage(queue, t, src):
            rows = src[0].rearrange("(a b r) c -> b r a c", a=2, b=2)
            for b in range(2):
                queue.dma_start(t[32 * b : 32 * b + 4, :, :].bitcast(I32), rows[b].bitcast(I32))

        def plane(name, width):
            t = tile(name, [P, width], U8)
            nc.vector.memset(t[:].bitcast(I32), 0)
            return t

        def load_plane(t, src):
            for q in range(4):
                nc.sync.dma_start(t[32 * q : 32 * q + 4, :].bitcast(I32), src[0, 4 * q : 4 * q + 4, :].bitcast(I32))

        w0s_raw = stage("w0s_raw", R, nc.gpsimd)
        ws_raw = stage("ws_raw", R, nc.vector)
        xos_win = plane("xos_win", Z)
        xts_win = plane("xts_win", T)
        load_stage(nc.gpsimd, w0s_raw, w0_scales)
        load_stage(nc.gpsimd, ws_raw, w_scales)

        ca_rows = ca.rearrange("(p t) v -> t p v", t=PACK)
        ca_win = [tile("ca_win%d" % t, [P, V], U8) for t in range(PACK)]
        nc.sync.dma_start(ca_win[0][:], ca_rows[0])
        sw_sb = tile("sw_sb", [P, PACK], F32)
        nc.scalar.dma_start(sw_sb[:], sw.rearrange("(p t) o -> p (t o)", t=PACK))
        l3 = load_list("l3", offs3, N // 16)
        for t in range(1, PACK):
            nc.sync.dma_start(ca_win[t][:], ca_rows[t])
        xo_win = tile("xo_win", [P, Z], U16)
        nc.sync.dma_start(xo_win[:].bitcast(I32), xo_words[0].bitcast(I32))
        w0_raw = tile("w0_raw", [P, R], U32)
        nc.sync.dma_start(w0_raw[:].bitcast(I32), w0_words[0].rearrange("p c r -> p (c r)").bitcast(I32))
        l2 = load_list("l2", offs2, J // 16)
        load_plane(xos_win, xo_scales)
        xt_win = tile("xt_win", [P, T], U32)
        nc.sync.dma_start(xt_win[:].bitcast(I32), xt_words[0].rearrange("p c r -> p (c r)").bitcast(I32))
        l1 = load_list("l1", offs, J // 16)
        w_raw = tile("w_raw", [P, R], U16)
        nc.sync.dma_start(w_raw[:].bitcast(I32), w_words[0].bitcast(I32))
        load_plane(xts_win, xt_scales)
        l4 = load_list("l4", offs4, O // 16)
        sa_sb = tile("sa_sb", [P, PACK], F32)
        nc.sync.dma_start(sa_sb[:], sa.rearrange("(p t) o -> p (t o)", t=PACK))

        def spread(name, raw, width, tag):
            t = tile(name, [P, width], U8, tag)
            for a in range(2):
                nc.vector.tensor_copy(t[64 * a : 64 * a + 64, :].bitcast(I32), raw[0:64, a, :].bitcast(I32))
            return t

        ca_got = tile("ca_got", [P, PACK, N], U8)
        wq4 = tile("wq4", [P, PACK, N], BF16)
        for t in range(PACK):
            nc.vector.tensor_copy(ca_got[:, t, :], ca_win[t][:].indirect(l3[:]))
            nc.scalar.activation(wq4[:, t, :], ca_got[:, t, :].bitcast(FP8), ACT.Copy, scale=sw_sb[:, t : t + 1])

        xts_got = tile("xts_got", [P, J], U8)
        xt_got = tile("xt_got", [P, J], U32)
        xo_got = tile("xo_got", [P, J], U16)
        xos_got = tile("xos_got", [P, J], U8)
        w0s_plane = spread("w0s_plane", w0s_raw, R, "ca_win3")
        nc.vector.tensor_copy(xo_got[:], xo_win[:].indirect(l2[:]))
        nc.vector.tensor_copy(xos_got[:], xos_win[:].indirect(l2[:]))
        ws_plane = spread("ws_plane", ws_raw, R, "xos_win")
        nc.vector.tensor_copy(xt_got[:], xt_win[:].indirect(l1[:]))
        nc.vector.tensor_copy(xts_got[:], xts_win[:].indirect(l1[:]))

        def deal(copy, name, raw, dtype, run):
            t = tile(name, [P, PACK, P], dtype)
            copy(t[:].rearrange("p t (c i) -> p c t i", i=run), raw.rearrange("p (c i t) -> p c t i", t=PACK, i=run))
            return t

        w0_d = deal(nc.scalar.copy, "w0_d", w0_raw[:], U32, 4)
        wq_il = tile("wq_il", [P, N, PACK], BF16, "w0_raw")
        nc.scalar.copy(wq_il[:], wq4[:].rearrange("p t n -> p n t"))
        w_d = deal(nc.scalar.copy, "w_d", w_raw[:], U16, 8)
        w0s_d = deal(nc.gpsimd.tensor_copy, "w0s_d", w0s_plane[:], U8, P)
        ws_d = deal(nc.gpsimd.tensor_copy, "ws_d", ws_plane[:], U8, P)

        acc = [ps.tile([P, J], F32, name="acc%d" % t) for t in range(PACK)]
        for t in range(PACK):
            nc.tensor.matmul_mx(acc[t][:], lhsT=w0_d[:, t, :].bitcast(E5M2X4), lhsT_scale=w0s_d[:, t, :],
                                rhs=xo_got[:].bitcast(E2M1X4), rhs_scale=xos_got[:], start=True, stop=False)
        for t in range(PACK):
            nc.tensor.matmul_mx(acc[t][:], lhsT=w_d[:, t, :].bitcast(E2M1X4), lhsT_scale=ws_d[:, t, :],
                                rhs=xt_got[:].bitcast(E4M3X4), rhs_scale=xts_got[:], start=False, stop=True)

        wq_codes = tile("wq_codes", [P, N], U32, "xts_win")
        wq_scales = tile("wq_scales", [P, N], U8)
        nc.vector.quantize_mx(wq_codes[:].bitcast(E4M3X4), wq_scales[:], wq_il[:].rearrange("p n t -> p (n t)"))

        hid4 = tile("hid4", [P, PACK, O], BF16)
        for t in range(PACK):
            g1 = tile("g1_%d" % t, [P, J], F32)
            nc.vector.tensor_scalar_max(g1[:], acc[t][:], 0.0)
            nc.scalar.activation(hid4[:, t, :], g1[:].indirect(l4[:]), ACT.Copy, scale=sa_sb[:, t : t + 1])
        hid_il = tile("hid_il", [P, O, PACK], BF16)
        nc.vector.tensor_copy(hid_il[:], hid4[:].rearrange("p t o -> p o t"))
        hid_codes = tile("hid_codes", [P, O], U32)
        hid_scales = tile("hid_scales", [P, O], U8)
        nc.vector.quantize_mx(hid_codes[:].bitcast(E4M3X4), hid_scales[:], hid_il[:].rearrange("p o t -> p (o t)"))

        for h, (copy, queue) in enumerate(((nc.vector.tensor_copy, nc.sync), (nc.scalar.copy, nc.scalar))):
            cols = slice(h * P, (h + 1) * P)
            res = ps.tile([P, O], F32, name="res%d" % h)
            nc.tensor.matmul_mx(res[:], lhsT=wq_codes[:, cols].bitcast(E4M3X4), lhsT_scale=wq_scales[:, cols],
                                rhs=hid_codes[:].bitcast(E4M3X4), rhs_scale=hid_scales[:], start=True, stop=True)
            res_sb = tile("res_sb%d" % h, [P, O], F32)
            copy(res_sb[:], res[:])
            queue.dma_start(out[cols, :], res_sb[:])
